import numpy as np
import ml_dtypes


def mxq(x, axis, fmt="e4m3"):
    dtype, down = {"e4m3": (ml_dtypes.float8_e4m3fn, 7), "e5m2": (ml_dtypes.float8_e5m2, 14)}[fmt]
    v = np.moveaxis(np.asarray(x, np.float32).astype(ml_dtypes.bfloat16).astype(np.float64), axis, -1)
    blocks = v.reshape(v.shape[:-1] + (-1, 32))
    amax = np.abs(blocks).max(-1, keepdims=True)
    byte = np.maximum(np.where(amax > 0, np.frexp(amax)[1] - 1 + 127, 0) - down, 1)
    scale = np.exp2(byte - 127.0)
    codes = (blocks / scale).astype(np.float32).astype(dtype).astype(np.float64)
    return np.moveaxis((codes * scale).reshape(v.shape), -1, axis)


WIDE = False


def mx_kscale(k):
    if not WIDE:
        return np.ones(k)
    levels = np.array([30, -30])
    if k % 512:
        return np.exp2(np.random.permutation(np.resize(levels, k // 32))).repeat(32)
    a = np.empty((k // 512, 16))
    for p in range(k // 512):
        a[p, :8] = np.random.permutation(np.resize(levels, 8))
        for g in range(8):
            far = levels[np.abs(levels - a[p, g]) >= 10]
            a[p, g + 8] = far[np.random.randint(len(far))]
    return np.exp2(a.ravel()).repeat(32)


def f64(x):
    return np.asarray(x).astype(np.float64)


def striped(idx):
    return np.tile(np.asarray(idx).reshape(-1, 16).T, (8, 1)).astype(np.uint16)


def unstriped(offs):
    return offs[:16].T.reshape(-1).astype(np.int64)


E2M1 = np.array([0.0, 0.5, 1.0, 1.5, 2.0, 3.0, 4.0, 6.0, -0.0, -0.5, -1.0, -1.5, -2.0, -3.0, -4.0, -6.0])


def pack_weight(w, fmt):
    k, n = w.shape
    w = f64(np.asarray(w, np.float32).astype(ml_dtypes.bfloat16)).reshape(k // 32, 32, n)
    amax = np.abs(w).max(1)
    if fmt in ("e4m3", "e5m2"):
        byte = np.frexp(amax)[1] - 1 + 127 - (7 if fmt == "e4m3" else 14)
    else:
        mant, ex = np.frexp(amax / 6.0)
        byte = np.where(mant > 0.5, ex, ex - 1) + 127
    byte = np.clip(np.where(amax > 0, byte, 1), 1, 254)
    scaled = (w * np.exp2(127.0 - byte)[:, None, :]).reshape(k, n).astype(np.float32)
    by_word = np.ascontiguousarray(scaled.reshape(k // 512, 128, 4, n).transpose(0, 1, 3, 2))
    if fmt in ("e4m3", "e5m2"):
        words = by_word.astype(ml_dtypes.float8_e4m3fn if fmt == "e4m3" else ml_dtypes.float8_e5m2).view(np.uint8)
    else:
        c = by_word.astype(ml_dtypes.float4_e2m1fn).view(np.uint8) & 0xF
        words = (c[..., 0::2] | (c[..., 1::2] << 4)).reshape(k // 512, 128, 2 * n)
    return np.ascontiguousarray(words), np.ascontiguousarray(byte.astype(np.uint8).reshape(k // 512, 16, n))


def unpack_weight(words, scales, fmt):
    g, _, n = scales.shape
    words = np.ascontiguousarray(words).reshape(g, 128, n, -1)
    if fmt in ("e4m3", "e5m2"):
        vals = words.view(ml_dtypes.float8_e4m3fn if fmt == "e4m3" else ml_dtypes.float8_e5m2).astype(np.float64)
    else:
        nib = np.empty((g, 128, n, 4), np.uint8)
        nib[..., 0::2] = words & 0xF
        nib[..., 1::2] = words >> 4
        vals = E2M1[nib]
    vals = vals * np.repeat(np.exp2(scales.astype(np.float64) - 127.0), 8, axis=1)[..., None]
    return vals.transpose(0, 1, 3, 2).reshape(g * 512, n)


def bf(x):
    return np.asarray(x, np.float32).astype(ml_dtypes.bfloat16)


def planes(Y):
    r, m = Y.shape
    b = f64(bf(Y)).reshape(r // 32, 32, m)
    amax = np.abs(b).max(1)
    byte = np.clip(np.where(amax > 0, np.frexp(amax)[1] - 1 + 127 - 7, 1), 1, 254)
    codes = (b * np.exp2(127.0 - byte)[:, None, :]).reshape(r, m).astype(np.float32).astype(ml_dtypes.float8_e4m3fn).view(np.uint8)
    words = codes.reshape(r // 512, 128, 4, m).transpose(0, 1, 3, 2)
    return np.ascontiguousarray(words), np.ascontiguousarray(byte.astype(np.uint8).reshape(r // 512, 16, m))


K, T, J, R, O, N, Z = 1024, 1024, 256, 512, 128, 512, 512


def setup_inputs():
    n = np.random.standard_normal
    idx = np.random.permutation(T)[:J]
    idx2 = np.random.permutation(T)[:J]
    idx3 = np.random.permutation(J)[:O]
    idx4 = np.random.permutation(Z)[:O]
    fk = mx_kscale(K)
    fr = mx_kscale(R)
    wp = pack_weight(n((K, R)) * 1 / np.sqrt(K) * fk[:, None] * fr, "e2m1")
    wbp = pack_weight(n((R, N)) * 1 / np.sqrt(R) / fr[:, None], "e5m2")
    return {
        "xf": (n((K, T))).astype(np.float32),
        "fk": (np.random.uniform(0.5, 2.0, (K, 1)) / fk[:, None]).astype(np.float32),
        "w_words": wp[0],
        "w_scales": wp[1],
        "wb_words": wbp[0],
        "wb_scales": wbp[1],
        "tz": (n((N, Z))).astype(np.float32),
        "offs": striped(idx),
        "offs2": striped(idx2),
        "offs3": striped(idx3),
        "offs4": striped(idx4),
    }


def reference(xf, fk, w_words, w_scales, wb_words, wb_scales, tz, offs, offs2, offs3, offs4):
    idx = unstriped(offs)
    idx2 = unstriped(offs2)
    idx3 = unstriped(offs3)
    idx4 = unstriped(offs4)
    wu = unpack_weight(w_words, w_scales, "e2m1")
    wbu = unpack_weight(wb_words, wb_scales, "e5m2")
    u = (f64(xf)[:, idx] - f64(xf)[:, idx2]) * f64(fk)
    uq = mxq(u, 0, "e4m3")
    a = wu.T @ uq
    ha = np.maximum(a, 0.0)
    hid = ha[:, idx3]
    hidq = mxq(hid, 0, "e5m2")
    p = wbu.T @ hidq
    y = p * f64(tz)[:, idx4]
    words, scales = planes(y)
    return y, words, scales

@@ -1,0 +1,183 @@
+from contextlib import ExitStack
+
+import concourse.mybir as mybir
+
+K, T, J, R, O, N, Z = 1024, 1024, 256, 512, 128, 512, 512
+FLOPS = 2 * K * R * J + 2 * R * N * O
+
+F32 = mybir.dt.float32
+BF16 = mybir.dt.bfloat16
+I32 = mybir.dt.int32
+U32 = mybir.dt.uint32
+U16 = mybir.dt.uint16
+U8 = mybir.dt.uint8
+E4M3 = mybir.dt.float8_e4m3fn_x4
+E5M2 = mybir.dt.float8_e5m2_x4
+E2M1 = mybir.dt.float4_e2m1fn_x4
+COPY = mybir.ActivationFunctionType.Copy
+RELU = mybir.ActivationFunctionType.Relu
+MULT = mybir.AluOpType.mult
+SUBTRACT = mybir.AluOpType.subtract
+
+P = 128
+PACK = 4
+PASSES = K // (P * PACK)
+
+
+def tile_list_pickgaps_relooked_timeslook_pl_kernel(
+    tc, xf, fk, w_words, w_scales, wb_words, wb_scales, tz, offs, offs2, offs3, offs4, out_0, out_1, out_2
+):
+    nc = tc.nc
+    with ExitStack() as ctx:
+        sb = ctx.enter_context(tc.tile_pool(name="sb", bufs=1))
+        ps = ctx.enter_context(tc.psum_pool(name="ps", bufs=1))
+
+        def tile(name, shape, dtype):
+            return sb.tile(shape, dtype, name=name, align_bytes=64)
+
+        lists = [tile("list%d" % i, list(src.shape), U16) for i, src in enumerate((offs, offs2, offs3, offs4))]
+        x_rows = xf.rearrange("(a p t) c -> a t p c", a=PASSES, t=PACK)
+        x = [[tile("x%d%d" % (a, t), [P, T], F32) for t in range(PACK)] for a in range(PASSES)]
+        fk_sb = tile("fk", [P, PASSES * PACK], F32)
+        w_raw = tile("w_raw", [P, PASSES, 2 * R], U8)
+        wb_raw = tile("wb_raw", [P, N], I32)
+        ws_raw = tile("ws_raw", [P, PASSES, R], U8)
+        wbs_raw = tile("wbs_raw", [P, N], U8)
+        tz_rows = tz.rearrange("(p t) z -> p t z", t=PACK)
+        tz_sb = [tile("tz%d" % h, [P, 2, Z], F32) for h in range(2)]
+
+        nc.vector.memset(ws_raw[:].bitcast(I32), 0)
+        nc.vector.memset(wbs_raw[:].bitcast(I32), 0)
+
+        nc.sync.dma_start(w_raw[:].bitcast(I32), w_words.rearrange("a p b -> p a b").bitcast(I32))
+        nc.sync.dma_start(x[0][0][:], x_rows[0, 0])
+        nc.sync.dma_start(lists[1][:], offs2)
+        nc.sync.dma_start(lists[0][:], offs)
+        nc.sync.dma_start(
+            fk_sb[:].rearrange("p (a t) -> p a t", t=PACK), fk.rearrange("(a p t) o -> p a (t o)", a=PASSES, t=PACK)
+        )
+        for t in range(1, PACK):
+            nc.sync.dma_start(x[0][t][:], x_rows[0, t])
+        for q in range(4):
+            nc.sync.dma_start(
+                ws_raw[32 * q : 32 * q + 4].bitcast(I32),
+                w_scales[:, 4 * q : 4 * q + 4, :].rearrange("a r c -> r a c").bitcast(I32),
+            )
+        for t in range(PACK):
+            nc.sync.dma_start(x[1][t][:], x_rows[1, t])
+        nc.sync.dma_start(lists[2][:], offs3)
+        nc.sync.dma_start(wb_raw[:], wb_words[0].rearrange("p c r -> p (c r)").bitcast(I32))
+        for q in range(4):
+            nc.sync.dma_start(
+                wbs_raw[32 * q : 32 * q + 4].bitcast(I32), wb_scales[0, 4 * q : 4 * q + 4, :].bitcast(I32)
+            )
+        for h in range(2):
+            nc.sync.dma_start(tz_sb[h][:], tz_rows[:, 2 * h : 2 * h + 2, :])
+        nc.sync.dma_start(lists[3][:], offs4)
+
+        w_dealt = tile("w_dealt", [P, PASSES, PACK, 2 * P], U8)
+        ws_dealt = tile("ws_dealt", [P, PASSES, PACK, P], U8)
+        wb_dealt = tile("wb_dealt", [P, PACK, P], I32)
+        wbs_dealt = tile("wbs_dealt", [P, PACK, P], U8)
+
+        acc = [ps.tile([P, J], F32, name="acc%d" % t) for t in range(PACK)]
+
+        def first_product(a, u_bf):
+            codes = tile("u_codes%d" % a, [P, J], U32)
+            scales = tile("u_scales%d" % a, [P, J], U8)
+            nc.vector.quantize_mx(codes[:].bitcast(E4M3), scales[:], u_bf[:].rearrange("p c t -> p (c t)"))
+            for t in range(PACK):
+                nc.tensor.matmul_mx(
+                    acc[t][:],
+                    lhsT=w_dealt[:, a, t, :].bitcast(E2M1),
+                    lhsT_scale=ws_dealt[:, a, t, :],
+                    rhs=codes[:].bitcast(E4M3),
+                    rhs_scale=scales[:],
+                    start=(a == 0),
+                    stop=(a == PASSES - 1),
+                )
+
+        def gap(a, t):
+            second = tile("second%d%d" % (a, t), [P, J], F32)
+            d = tile("gap%d%d" % (a, t), [P, J], F32)
+            nc.scalar.activation(second[:], x[a][t][:].indirect(lists[1][:]), COPY)
+            nc.vector.tensor_tensor(d[:], x[a][t][:].indirect(lists[0][:]), second[:], SUBTRACT)
+            return d
+
+        def factor(a, t):
+            return fk_sb[:, PACK * a + t : PACK * a + t + 1]
+
+        nc.vector.tensor_copy(
+            w_dealt[:].bitcast(U16), w_raw[:].bitcast(U16).rearrange("p a (m t) -> p a t m", t=PACK)
+        )
+        u_planes = tile("u_planes", [P, PACK, J], BF16)
+        u0 = tile("u0", [P, J, PACK], BF16)
+        for t in range(PACK):
+            d = gap(0, t)
+            nc.scalar.activation(u_planes[:, t, :], d[:], COPY, scale=factor(0, t))
+        nc.vector.tensor_copy(
+            u0[:].rearrange("p (c i) t -> p c t i", i=4), u_planes[:].rearrange("p t (c i) -> p c t i", i=4)
+        )
+        nc.vector.tensor_copy(ws_dealt[:], ws_raw[:].rearrange("p a (m t) -> p a t m", t=PACK))
+        first_product(0, u0)
+
+        u1 = tile("u1", [P, J, PACK], BF16)
+        for t in range(2):
+            d = gap(1, t)
+            nc.scalar.activation(u1[:, :, t], d[:], COPY, scale=factor(1, t))
+        d = gap(1, 2)
+        nc.vector.tensor_scalar_mul(u1[:, :, 2], d[:], factor(1, 2))
+        first = tile("first", [P, J], F32)
+        second = tile("second", [P, J], F32)
+        d = tile("gap", [P, J], F32)
+        nc.scalar.activation(second[:], x[1][3][:].indirect(lists[1][:]), COPY)
+        nc.vector.tensor_copy(first[:], x[1][3][:].indirect(lists[0][:]))
+        nc.vector.tensor_tensor(d[:], first[:], second[:], SUBTRACT)
+        nc.vector.tensor_scalar_mul(u1[:, :, 3], d[:], factor(1, 3))
+        first_product(1, u1)
+        nc.vector.tensor_copy(wbs_dealt[:], wbs_raw[:].rearrange("p (m t) -> p t m", t=PACK))
+        nc.vector.tensor_copy(
+            wb_dealt[:].rearrange("p t (c i) -> p c t i", i=4), wb_raw[:].rearrange("p (c i t) -> p c t i", i=4, t=PACK)
+        )
+
+        hid = tile("hid", [P, O, PACK], BF16)
+        for t in range(PACK):
+            ha = tile("ha%d" % t, [P, J], F32)
+            nc.scalar.activation(ha[:], acc[t][:], RELU)
+            nc.vector.tensor_copy(hid[:, :, t], ha[:].indirect(lists[2][:]))
+        h_codes = tile("h_codes", [P, O], U32)
+        h_scales = tile("h_scales", [P, O], U8)
+        nc.vector.quantize_mx(h_codes[:].bitcast(E5M2), h_scales[:], hid[:].rearrange("p c t -> p (c t)"))
+
+        tz_picked = tile("tz_picked", [P, PACK, O], F32)
+        for t in range(PACK):
+            nc.scalar.activation(tz_picked[:, t, :], tz_sb[t // 2][:, t % 2, :].indirect(lists[3][:]), COPY)
+
+        y = tile("y", [P, PACK, O], F32)
+        y_rows = out_0.rearrange("(p t) o -> p t o", t=PACK)
+        for h in range(2):
+            prod = ps.tile([P, 2, O], F32, name="prod%d" % h)
+            for s in range(2):
+                t = 2 * h + s
+                nc.tensor.matmul_mx(
+                    prod[:, s, :],
+                    lhsT=wb_dealt[:, t, :].bitcast(E5M2),
+                    lhsT_scale=wbs_dealt[:, t, :],
+                    rhs=h_codes[:].bitcast(E5M2),
+                    rhs_scale=h_scales[:],
+                    start=True,
+                    stop=True,
+                )
+            nc.vector.tensor_tensor(y[:, 2 * h : 2 * h + 2, :], prod[:], tz_picked[:, 2 * h : 2 * h + 2, :], MULT)
+        nc.sync.dma_start(y_rows, y[:])
+        y_bf = tile("y_bf", [P, O, PACK], BF16)
+        nc.vector.tensor_copy(
+            y_bf[:].rearrange("p (c i) t -> p c t i", i=4), y[:].rearrange("p t (c i) -> p c t i", i=4)
+        )
+        y_codes = tile("y_codes", [P, O], U32)
+        y_scales = tile("y_scales", [P, O], U8)
+        nc.vector.quantize_mx(y_codes[:].bitcast(E4M3), y_scales[:], y_bf[:].rearrange("p c t -> p (c t)"))
+        nc.sync.dma_start(out_1[0].rearrange("p c r -> p (c r)").bitcast(I32), y_codes[:].bitcast(I32))
+        for q in range(4):
+            queue = nc.scalar if q % 2 == 0 else nc.sync
+            queue.dma_start(out_2[0, 4 * q : 4 * q + 4, :].bitcast(I32), y_scales[32 * q : 32 * q + 4, :].bitcast(I32))

@@ -30,6 +30,7 @@ def tile_list_pickgaps_relooked_timeslook_pl_kernel(
     nc = tc.nc
     with ExitStack() as ctx:
         sb = ctx.enter_context(tc.tile_pool(name="sb", bufs=1))
+        shared = ctx.enter_context(tc.tile_pool(name="shared", bufs=1))
         ps = ctx.enter_context(tc.psum_pool(name="ps", bufs=1))
 
         def tile(name, shape, dtype):
@@ -46,46 +47,53 @@ def tile_list_pickgaps_relooked_timeslook_pl_kernel(
         tz_rows = tz.rearrange("(p t) z -> p t z", t=PACK)
         tz_sb = [tile("tz%d" % h, [P, 2, Z], F32) for h in range(2)]
 
-        nc.vector.memset(ws_raw[:].bitcast(I32), 0)
-        nc.vector.memset(wbs_raw[:].bitcast(I32), 0)
+        nc.gpsimd.memset(ws_raw[:].bitcast(I32), 0)
+        nc.gpsimd.memset(wbs_raw[:].bitcast(I32), 0)
 
-        nc.sync.dma_start(w_raw[:].bitcast(I32), w_words.rearrange("a p b -> p a b").bitcast(I32))
-        nc.sync.dma_start(x[0][0][:], x_rows[0, 0])
+        nc.scalar.dma_start(ws_raw[0 : 4].bitcast(I32), w_scales[:, 0 : 4, :].rearrange("a r c -> r a c").bitcast(I32))
+        nc.scalar.dma_start(ws_raw[32 : 36].bitcast(I32), w_scales[:, 4 : 8, :].rearrange("a r c -> r a c").bitcast(I32))
+        nc.scalar.dma_start(ws_raw[64 : 68].bitcast(I32), w_scales[:, 8 : 12, :].rearrange("a r c -> r a c").bitcast(I32))
+        nc.scalar.dma_start(ws_raw[96 : 100].bitcast(I32), w_scales[:, 12 : 16, :].rearrange("a r c -> r a c").bitcast(I32))
         nc.sync.dma_start(lists[1][:], offs2)
+        nc.sync.dma_start(x[0][0][:], x_rows[0, 0])
         nc.sync.dma_start(lists[0][:], offs)
-        nc.sync.dma_start(
-            fk_sb[:].rearrange("p (a t) -> p a t", t=PACK), fk.rearrange("(a p t) o -> p a (t o)", a=PASSES, t=PACK)
-        )
-        for t in range(1, PACK):
-            nc.sync.dma_start(x[0][t][:], x_rows[0, t])
-        for q in range(4):
-            nc.sync.dma_start(
-                ws_raw[32 * q : 32 * q + 4].bitcast(I32),
-                w_scales[:, 4 * q : 4 * q + 4, :].rearrange("a r c -> r a c").bitcast(I32),
-            )
-        for t in range(PACK):
-            nc.sync.dma_start(x[1][t][:], x_rows[1, t])
-        nc.sync.dma_start(lists[2][:], offs3)
+        nc.sync.dma_start(w_raw[:].bitcast(I32), w_words.rearrange("a p b -> p a b").bitcast(I32))
+        nc.sync.dma_start(x[0][1][:], x_rows[0, 1])
+        nc.sync.dma_start(fk_sb[:].rearrange("p (a t) -> p a t", t=PACK), fk.rearrange("(a p t) o -> p a (t o)", a=PASSES, t=PACK))
+        nc.sync.dma_start(x[0][2][:], x_rows[0, 2])
+        nc.sync.dma_start(x[0][3][:], x_rows[0, 3])
+        nc.sync.dma_start(x[1][0][:], x_rows[1, 0])
+        nc.sync.dma_start(x[1][1][:], x_rows[1, 1])
+        nc.sync.dma_start(wbs_raw[0 : 4].bitcast(I32), wb_scales[0, 0 : 4, :].bitcast(I32))
+        nc.sync.dma_start(wbs_raw[32 : 36].bitcast(I32), wb_scales[0, 4 : 8, :].bitcast(I32))
+        nc.sync.dma_start(wbs_raw[64 : 68].bitcast(I32), wb_scales[0, 8 : 12, :].bitcast(I32))
+        nc.sync.dma_start(wbs_raw[96 : 100].bitcast(I32), wb_scales[0, 12 : 16, :].bitcast(I32))
+        nc.sync.dma_start(x[1][2][:], x_rows[1, 2])
+        nc.sync.dma_start(x[1][3][:], x_rows[1, 3])
         nc.sync.dma_start(wb_raw[:], wb_words[0].rearrange("p c r -> p (c r)").bitcast(I32))
-        for q in range(4):
-            nc.sync.dma_start(
-                wbs_raw[32 * q : 32 * q + 4].bitcast(I32), wb_scales[0, 4 * q : 4 * q + 4, :].bitcast(I32)
-            )
-        for h in range(2):
-            nc.sync.dma_start(tz_sb[h][:], tz_rows[:, 2 * h : 2 * h + 2, :])
+        nc.sync.dma_start(lists[2][:], offs3)
+        nc.sync.dma_start(tz_sb[0][:], tz_rows[:, 0 : 2, :])
+        nc.sync.dma_start(tz_sb[1][:], tz_rows[:, 2 : 4, :])
         nc.sync.dma_start(lists[3][:], offs4)
 
+        warm = tile("warm", [P, 16], F32)
+        nc.gpsimd.memset(warm[:, 0:8], 0.0)
+        nc.scalar.activation(warm[:, 8:16], warm[:, 0:8], COPY)
         w_dealt = tile("w_dealt", [P, PASSES, PACK, 2 * P], U8)
         ws_dealt = tile("ws_dealt", [P, PASSES, PACK, P], U8)
-        wb_dealt = tile("wb_dealt", [P, PACK, P], I32)
-        wbs_dealt = tile("wbs_dealt", [P, PACK, P], U8)
 
         acc = [ps.tile([P, J], F32, name="acc%d" % t) for t in range(PACK)]
 
-        def first_product(a, u_bf):
+        halves = [slice(0, J // 2), slice(J // 2, J)]
+        list_halves = [slice(0, J // 32), slice(J // 32, J // 16)]
+
+        def first_product(a, u_halves):
             codes = tile("u_codes%d" % a, [P, J], U32)
             scales = tile("u_scales%d" % a, [P, J], U8)
-            nc.vector.quantize_mx(codes[:].bitcast(E4M3), scales[:], u_bf[:].rearrange("p c t -> p (c t)"))
+            for cols, u_bf in zip(halves, u_halves):
+                nc.vector.quantize_mx(
+                    codes[:, cols].bitcast(E4M3), scales[:, cols], u_bf[:].rearrange("p c t -> p (c t)")
+                )
             for t in range(PACK):
                 nc.tensor.matmul_mx(
                     acc[t][:],
@@ -100,8 +108,21 @@ def tile_list_pickgaps_relooked_timeslook_pl_kernel(
         def gap(a, t):
             second = tile("second%d%d" % (a, t), [P, J], F32)
             d = tile("gap%d%d" % (a, t), [P, J], F32)
-            nc.scalar.activation(second[:], x[a][t][:].indirect(lists[1][:]), COPY)
-            nc.vector.tensor_tensor(d[:], x[a][t][:].indirect(lists[0][:]), second[:], SUBTRACT)
+            if (a, t) in ((0, 1), (0, 3), (1, 1)):
+                first = tile("first%d%d" % (a, t), [P, J], F32)
+                for cols, ent in zip(halves, list_halves):
+                    nc.scalar.activation(second[:, cols], x[a][t][:].indirect(lists[1][:, ent]), COPY)
+                    nc.scalar.activation(first[:, cols], x[a][t][:].indirect(lists[0][:, ent]), COPY)
+                for cols in halves:
+                    nc.vector.tensor_tensor(d[:, cols], first[:, cols], second[:, cols], SUBTRACT)
+            else:
+                if (a, t) in [(i, j) for i in range(2) for j in range(4)]:
+                    for cols, ent in zip(halves, list_halves):
+                        nc.scalar.activation(second[:, cols], x[a][t][:].indirect(lists[1][:, ent]), COPY)
+                else:
+                    nc.scalar.activation(second[:], x[a][t][:].indirect(lists[1][:]), COPY)
+                for cols, ent in zip(halves, list_halves):
+                    nc.vector.tensor_tensor(d[:, cols], x[a][t][:].indirect(lists[0][:, ent]), second[:, cols], SUBTRACT)
             return d
 
         def factor(a, t):
@@ -110,31 +131,25 @@ def tile_list_pickgaps_relooked_timeslook_pl_kernel(
         nc.vector.tensor_copy(
             w_dealt[:].bitcast(U16), w_raw[:].bitcast(U16).rearrange("p a (m t) -> p a t m", t=PACK)
         )
-        u_planes = tile("u_planes", [P, PACK, J], BF16)
-        u0 = tile("u0", [P, J, PACK], BF16)
-        for t in range(PACK):
-            d = gap(0, t)
-            nc.scalar.activation(u_planes[:, t, :], d[:], COPY, scale=factor(0, t))
-        nc.vector.tensor_copy(
-            u0[:].rearrange("p (c i) t -> p c t i", i=4), u_planes[:].rearrange("p t (c i) -> p c t i", i=4)
-        )
         nc.vector.tensor_copy(ws_dealt[:], ws_raw[:].rearrange("p a (m t) -> p a t m", t=PACK))
-        first_product(0, u0)
-
-        u1 = tile("u1", [P, J, PACK], BF16)
-        for t in range(2):
-            d = gap(1, t)
-            nc.scalar.activation(u1[:, :, t], d[:], COPY, scale=factor(1, t))
-        d = gap(1, 2)
-        nc.vector.tensor_scalar_mul(u1[:, :, 2], d[:], factor(1, 2))
-        first = tile("first", [P, J], F32)
-        second = tile("second", [P, J], F32)
-        d = tile("gap", [P, J], F32)
-        nc.scalar.activation(second[:], x[1][3][:].indirect(lists[1][:]), COPY)
-        nc.vector.tensor_copy(first[:], x[1][3][:].indirect(lists[0][:]))
-        nc.vector.tensor_tensor(d[:], first[:], second[:], SUBTRACT)
-        nc.vector.tensor_scalar_mul(u1[:, :, 3], d[:], factor(1, 3))
-        first_product(1, u1)
+        for a in range(PASSES):
+            pairs = [tile("pairs%d%d" % (a, h), [P, 2, J // 2, 2], BF16) for h in range(2)]
+            for t in range(PACK):
+                d = gap(a, t)
+                for h, cols in enumerate(halves):
+                    nc.vector.tensor_scalar_mul(pairs[h][:, t // 2, :, t % 2], d[:, cols], factor(a, t))
+            u = []
+            for h in range(2):
+                if a == 0:
+                    u.append(tile("u0%d" % h, [P, J // 2, PACK], BF16))
+                else:
+                    u.append(shared.tile([P, J // 2, PACK], BF16, name="u1%d" % h, align_bytes=64, offset=512 + 1024 * h))
+                nc.vector.tensor_copy(
+                    u[h][:].bitcast(I32), pairs[h][:].bitcast(I32).rearrange("p s c o -> p c (s o)")
+                )
+            first_product(a, u)
+        wb_dealt = shared.tile([P, PACK, P], I32, name="wb_dealt", align_bytes=64, offset=0)
+        wbs_dealt = shared.tile([P, PACK, P], U8, name="wbs_dealt", align_bytes=64, offset=2048)
         nc.vector.tensor_copy(wbs_dealt[:], wbs_raw[:].rearrange("p (m t) -> p t m", t=PACK))
         nc.vector.tensor_copy(
             wb_dealt[:].rearrange("p t (c i) -> p c t i", i=4), wb_raw[:].rearrange("p (c i t) -> p c t i", i=4, t=PACK)
@@ -153,7 +168,7 @@ def tile_list_pickgaps_relooked_timeslook_pl_kernel(
         for t in range(PACK):
             nc.scalar.activation(tz_picked[:, t, :], tz_sb[t // 2][:, t % 2, :].indirect(lists[3][:]), COPY)
 
-        y = tile("y", [P, PACK, O], F32)
+        y_bf = tile("y_bf", [P, O, PACK], BF16)
         y_rows = out_0.rearrange("(p t) o -> p t o", t=PACK)
         for h in range(2):
             prod = ps.tile([P, 2, O], F32, name="prod%d" % h)
@@ -168,12 +183,13 @@ def tile_list_pickgaps_relooked_timeslook_pl_kernel(
                     start=True,
                     stop=True,
                 )
-            nc.vector.tensor_tensor(y[:, 2 * h : 2 * h + 2, :], prod[:], tz_picked[:, 2 * h : 2 * h + 2, :], MULT)
-        nc.sync.dma_start(y_rows, y[:])
-        y_bf = tile("y_bf", [P, O, PACK], BF16)
-        nc.vector.tensor_copy(
-            y_bf[:].rearrange("p (c i) t -> p c t i", i=4), y[:].rearrange("p t (c i) -> p c t i", i=4)
-        )
+            y = tile("y%d" % h, [P, 2, O], F32)
+            nc.vector.tensor_tensor(y[:], prod[:], tz_picked[:, 2 * h : 2 * h + 2, :], MULT)
+            nc.sync.dma_start(y_rows[:, 2 * h : 2 * h + 2, :], y[:])
+            if h == 0:
+                nc.scalar.copy(y_bf[:, :, 0:2], y[:].rearrange("p s c -> p c s"))
+            else:
+                nc.vector.tensor_copy(y_bf[:, :, 2:4], y[:].rearrange("p s c -> p c s"))
         y_codes = tile("y_codes", [P, O], U32)
         y_scales = tile("y_scales", [P, O], U8)
         nc.vector.quantize_mx(y_codes[:].bitcast(E4M3), y_scales[:], y_bf[:].rearrange("p c t -> p (c t)"))

@@ -50,14 +50,14 @@ def tile_list_pickgaps_relooked_timeslook_pl_kernel(
         nc.gpsimd.memset(ws_raw[:].bitcast(I32), 0)
         nc.gpsimd.memset(wbs_raw[:].bitcast(I32), 0)
 
-        nc.scalar.dma_start(ws_raw[0 : 4].bitcast(I32), w_scales[:, 0 : 4, :].rearrange("a r c -> r a c").bitcast(I32))
-        nc.scalar.dma_start(ws_raw[32 : 36].bitcast(I32), w_scales[:, 4 : 8, :].rearrange("a r c -> r a c").bitcast(I32))
-        nc.scalar.dma_start(ws_raw[64 : 68].bitcast(I32), w_scales[:, 8 : 12, :].rearrange("a r c -> r a c").bitcast(I32))
-        nc.scalar.dma_start(ws_raw[96 : 100].bitcast(I32), w_scales[:, 12 : 16, :].rearrange("a r c -> r a c").bitcast(I32))
         nc.sync.dma_start(lists[1][:], offs2)
+        nc.sync.dma_start(w_raw[:].bitcast(I32), w_words.rearrange("a p b -> p a b").bitcast(I32))
+        nc.sync.dma_start(ws_raw[0 : 4].bitcast(I32), w_scales[:, 0 : 4, :].rearrange("a r c -> r a c").bitcast(I32))
+        nc.sync.dma_start(ws_raw[32 : 36].bitcast(I32), w_scales[:, 4 : 8, :].rearrange("a r c -> r a c").bitcast(I32))
+        nc.sync.dma_start(ws_raw[64 : 68].bitcast(I32), w_scales[:, 8 : 12, :].rearrange("a r c -> r a c").bitcast(I32))
+        nc.sync.dma_start(ws_raw[96 : 100].bitcast(I32), w_scales[:, 12 : 16, :].rearrange("a r c -> r a c").bitcast(I32))
         nc.sync.dma_start(x[0][0][:], x_rows[0, 0])
         nc.sync.dma_start(lists[0][:], offs)
-        nc.sync.dma_start(w_raw[:].bitcast(I32), w_words.rearrange("a p b -> p a b").bitcast(I32))
         nc.sync.dma_start(x[0][1][:], x_rows[0, 1])
         nc.sync.dma_start(fk_sb[:].rearrange("p (a t) -> p a t", t=PACK), fk.rearrange("(a p t) o -> p a (t o)", a=PASSES, t=PACK))
         nc.sync.dma_start(x[0][2][:], x_rows[0, 2])
@@ -68,13 +68,13 @@ def tile_list_pickgaps_relooked_timeslook_pl_kernel(
         nc.sync.dma_start(wbs_raw[32 : 36].bitcast(I32), wb_scales[0, 4 : 8, :].bitcast(I32))
         nc.sync.dma_start(wbs_raw[64 : 68].bitcast(I32), wb_scales[0, 8 : 12, :].bitcast(I32))
         nc.sync.dma_start(wbs_raw[96 : 100].bitcast(I32), wb_scales[0, 12 : 16, :].bitcast(I32))
+        nc.sync.dma_start(lists[3][:], offs4)
         nc.sync.dma_start(x[1][2][:], x_rows[1, 2])
         nc.sync.dma_start(x[1][3][:], x_rows[1, 3])
         nc.sync.dma_start(wb_raw[:], wb_words[0].rearrange("p c r -> p (c r)").bitcast(I32))
-        nc.sync.dma_start(lists[2][:], offs3)
         nc.sync.dma_start(tz_sb[0][:], tz_rows[:, 0 : 2, :])
+        nc.sync.dma_start(lists[2][:], offs3)
         nc.sync.dma_start(tz_sb[1][:], tz_rows[:, 2 : 4, :])
-        nc.sync.dma_start(lists[3][:], offs4)
 
         warm = tile("warm", [P, 16], F32)
         nc.gpsimd.memset(warm[:, 0:8], 0.0)
@@ -94,21 +94,23 @@ def tile_list_pickgaps_relooked_timeslook_pl_kernel(
                 nc.vector.quantize_mx(
                     codes[:, cols].bitcast(E4M3), scales[:, cols], u_bf[:].rearrange("p c t -> p (c t)")
                 )
+            ranges = [slice(0, J)] if a == 0 else halves
             for t in range(PACK):
-                nc.tensor.matmul_mx(
-                    acc[t][:],
-                    lhsT=w_dealt[:, a, t, :].bitcast(E2M1),
-                    lhsT_scale=ws_dealt[:, a, t, :],
-                    rhs=codes[:].bitcast(E4M3),
-                    rhs_scale=scales[:],
-                    start=(a == 0),
-                    stop=(a == PASSES - 1),
-                )
+                for cols in ranges:
+                    nc.tensor.matmul_mx(
+                        acc[t][:, cols],
+                        lhsT=w_dealt[:, a, t, :].bitcast(E2M1),
+                        lhsT_scale=ws_dealt[:, a, t, :],
+                        rhs=codes[:, cols].bitcast(E4M3),
+                        rhs_scale=scales[:, cols],
+                        start=(a == 0),
+                        stop=(a == PASSES - 1 and cols.stop == J),
+                    )
 
         def gap(a, t):
             second = tile("second%d%d" % (a, t), [P, J], F32)
             d = tile("gap%d%d" % (a, t), [P, J], F32)
-            if (a, t) in ((0, 1), (0, 3), (1, 1)):
+            if (a, t) in ((1, 0),):
                 first = tile("first%d%d" % (a, t), [P, J], F32)
                 for cols, ent in zip(halves, list_halves):
                     nc.scalar.activation(second[:, cols], x[a][t][:].indirect(lists[1][:, ent]), COPY)
@@ -168,31 +170,34 @@ def tile_list_pickgaps_relooked_timeslook_pl_kernel(
         for t in range(PACK):
             nc.scalar.activation(tz_picked[:, t, :], tz_sb[t // 2][:, t % 2, :].indirect(lists[3][:]), COPY)
 
-        y_bf = tile("y_bf", [P, O, PACK], BF16)
+        y = [tile("y%d" % h, [P, 2, O], F32) for h in range(2)]
         y_rows = out_0.rearrange("(p t) o -> p t o", t=PACK)
-        for h in range(2):
-            prod = ps.tile([P, 2, O], F32, name="prod%d" % h)
-            for s in range(2):
-                t = 2 * h + s
-                nc.tensor.matmul_mx(
-                    prod[:, s, :],
-                    lhsT=wb_dealt[:, t, :].bitcast(E5M2),
-                    lhsT_scale=wbs_dealt[:, t, :],
-                    rhs=h_codes[:].bitcast(E5M2),
-                    rhs_scale=h_scales[:],
-                    start=True,
-                    stop=True,
-                )
-            y = tile("y%d" % h, [P, 2, O], F32)
-            nc.vector.tensor_tensor(y[:], prod[:], tz_picked[:, 2 * h : 2 * h + 2, :], MULT)
-            nc.sync.dma_start(y_rows[:, 2 * h : 2 * h + 2, :], y[:])
-            if h == 0:
-                nc.scalar.copy(y_bf[:, :, 0:2], y[:].rearrange("p s c -> p c s"))
-            else:
-                nc.vector.tensor_copy(y_bf[:, :, 2:4], y[:].rearrange("p s c -> p c s"))
+        o_halves = [slice(0, O // 2), slice(O // 2, O)]
+        y_bf = [tile("y_bf%d" % h, [P, O // 2, PACK], BF16) for h in range(2)]
+        for t in range(PACK):
+            prod = ps.tile([P, O], F32, name="prod%d" % t)
+            nc.tensor.matmul_mx(
+                prod[:],
+                lhsT=wb_dealt[:, t, :].bitcast(E5M2),
+                lhsT_scale=wbs_dealt[:, t, :],
+                rhs=h_codes[:].bitcast(E5M2),
+                rhs_scale=h_scales[:],
+                start=True,
+                stop=True,
+            )
+            for cols in o_halves if t == PACK - 1 else [slice(0, O)]:
+                nc.vector.tensor_tensor(y[t // 2][:, t % 2, cols], prod[:, cols], tz_picked[:, t, cols], MULT)
+            if t % 2 == 1:
+                nc.sync.dma_start(y_rows[:, t - 1 : t + 1, :], y[t // 2][:])
+                copy = nc.scalar.copy if t == 1 else nc.vector.tensor_copy
+                for h, cols in enumerate(o_halves):
+                    copy(y_bf[h][:, :, t - 1 : t + 1], y[t // 2][:, :, cols].rearrange("p s c -> p c s"))
         y_codes = tile("y_codes", [P, O], U32)
         y_scales = tile("y_scales", [P, O], U8)
-        nc.vector.quantize_mx(y_codes[:].bitcast(E4M3), y_scales[:], y_bf[:].rearrange("p c t -> p (c t)"))
+        for h, cols in enumerate(o_halves):
+            nc.vector.quantize_mx(
+                y_codes[:, cols].bitcast(E4M3), y_scales[:, cols], y_bf[h][:].rearrange("p c t -> p (c t)")
+            )
         nc.sync.dma_start(out_1[0].rearrange("p c r -> p (c r)").bitcast(I32), y_codes[:].bitcast(I32))
         for q in range(4):
             queue = nc.scalar if q % 2 == 0 else nc.sync

@@ -39,7 +39,7 @@ def tile_list_pickgaps_relooked_timeslook_pl_kernel(
         lists = [tile("list%d" % i, list(src.shape), U16) for i, src in enumerate((offs, offs2, offs3, offs4))]
         x_rows = xf.rearrange("(a p t) c -> a t p c", a=PASSES, t=PACK)
         x = [[tile("x%d%d" % (a, t), [P, T], F32) for t in range(PACK)] for a in range(PASSES)]
-        fk_sb = tile("fk", [P, PASSES * PACK], F32)
+        fk_sb = tile("fk", [P, PASSES, 2 * PACK], F32)
         w_raw = tile("w_raw", [P, PASSES, 2 * R], U8)
         wb_raw = tile("wb_raw", [P, N], I32)
         ws_raw = tile("ws_raw", [P, PASSES, R], U8)
@@ -50,6 +50,8 @@ def tile_list_pickgaps_relooked_timeslook_pl_kernel(
         nc.gpsimd.memset(ws_raw[:].bitcast(I32), 0)
         nc.gpsimd.memset(wbs_raw[:].bitcast(I32), 0)
 
+        warm = tile("warm", [P, 1], F32)
+        nc.scalar.activation(warm[:], wbs_raw[:, 0:4].bitcast(F32), COPY)
         nc.sync.dma_start(lists[1][:], offs2)
         nc.sync.dma_start(w_raw[:].bitcast(I32), w_words.rearrange("a p b -> p a b").bitcast(I32))
         nc.sync.dma_start(ws_raw[0 : 4].bitcast(I32), w_scales[:, 0 : 4, :].rearrange("a r c -> r a c").bitcast(I32))
@@ -59,7 +61,7 @@ def tile_list_pickgaps_relooked_timeslook_pl_kernel(
         nc.sync.dma_start(x[0][0][:], x_rows[0, 0])
         nc.sync.dma_start(lists[0][:], offs)
         nc.sync.dma_start(x[0][1][:], x_rows[0, 1])
-        nc.sync.dma_start(fk_sb[:].rearrange("p (a t) -> p a t", t=PACK), fk.rearrange("(a p t) o -> p a (t o)", a=PASSES, t=PACK))
+        nc.sync.dma_start(fk_sb[:, :, 0:PACK], fk.rearrange("(a p t) o -> p a (t o)", a=PASSES, t=PACK))
         nc.sync.dma_start(x[0][2][:], x_rows[0, 2])
         nc.sync.dma_start(x[0][3][:], x_rows[0, 3])
         nc.sync.dma_start(x[1][0][:], x_rows[1, 0])
@@ -76,9 +78,6 @@ def tile_list_pickgaps_relooked_timeslook_pl_kernel(
         nc.sync.dma_start(lists[2][:], offs3)
         nc.sync.dma_start(tz_sb[1][:], tz_rows[:, 2 : 4, :])
 
-        warm = tile("warm", [P, 16], F32)
-        nc.gpsimd.memset(warm[:, 0:8], 0.0)
-        nc.scalar.activation(warm[:, 8:16], warm[:, 0:8], COPY)
         w_dealt = tile("w_dealt", [P, PASSES, PACK, 2 * P], U8)
         ws_dealt = tile("ws_dealt", [P, PASSES, PACK, P], U8)
 
@@ -110,25 +109,19 @@ def tile_list_pickgaps_relooked_timeslook_pl_kernel(
         def gap(a, t):
             second = tile("second%d%d" % (a, t), [P, J], F32)
             d = tile("gap%d%d" % (a, t), [P, J], F32)
-            if (a, t) in ((1, 0),):
-                first = tile("first%d%d" % (a, t), [P, J], F32)
-                for cols, ent in zip(halves, list_halves):
-                    nc.scalar.activation(second[:, cols], x[a][t][:].indirect(lists[1][:, ent]), COPY)
-                    nc.scalar.activation(first[:, cols], x[a][t][:].indirect(lists[0][:, ent]), COPY)
-                for cols in halves:
-                    nc.vector.tensor_tensor(d[:, cols], first[:, cols], second[:, cols], SUBTRACT)
+            for cols, ent in zip(halves, list_halves):
+                nc.scalar.activation(second[:, cols], x[a][t][:].indirect(lists[1][:, ent]), COPY)
+            nc.vector.tensor_tensor(d[:, halves[0]], x[a][t][:].indirect(lists[0][:, list_halves[0]]), second[:, halves[0]], SUBTRACT)
+            if (a, t) in ((1, 0), (1, 1)):
+                first = tile("first%d%d" % (a, t), [P, J // 2], F32)
+                nc.scalar.activation(first[:], x[a][t][:].indirect(lists[0][:, list_halves[1]]), COPY)
+                nc.vector.tensor_tensor(d[:, halves[1]], first[:], second[:, halves[1]], SUBTRACT)
             else:
-                if (a, t) in [(i, j) for i in range(2) for j in range(4)]:
-                    for cols, ent in zip(halves, list_halves):
-                        nc.scalar.activation(second[:, cols], x[a][t][:].indirect(lists[1][:, ent]), COPY)
-                else:
-                    nc.scalar.activation(second[:], x[a][t][:].indirect(lists[1][:]), COPY)
-                for cols, ent in zip(halves, list_halves):
-                    nc.vector.tensor_tensor(d[:, cols], x[a][t][:].indirect(lists[0][:, ent]), second[:, cols], SUBTRACT)
+                nc.vector.tensor_tensor(d[:, halves[1]], x[a][t][:].indirect(lists[0][:, list_halves[1]]), second[:, halves[1]], SUBTRACT)
             return d
 
         def factor(a, t):
-            return fk_sb[:, PACK * a + t : PACK * a + t + 1]
+            return fk_sb[:, a, t : t + 1]
 
         nc.vector.tensor_copy(
             w_dealt[:].bitcast(U16), w_raw[:].bitcast(U16).rearrange("p a (m t) -> p a t m", t=PACK)
@@ -157,22 +150,42 @@ def tile_list_pickgaps_relooked_timeslook_pl_kernel(
             wb_dealt[:].rearrange("p t (c i) -> p c t i", i=4), wb_raw[:].rearrange("p (c i t) -> p c t i", i=4, t=PACK)
         )
 
-        hid = tile("hid", [P, O, PACK], BF16)
+        o_halves = [slice(0, O // 2), slice(O // 2, O)]
+        picked = tile("picked", [P, PACK, O], F32)
+        ha = [tile("ha%d" % t, [P, J], F32) for t in range(PACK - 1)]
+        ha.append(shared.tile([P, J], F32, name="ha3", align_bytes=64, offset=4096))
         for t in range(PACK):
-            ha = tile("ha%d" % t, [P, J], F32)
-            nc.scalar.activation(ha[:], acc[t][:], RELU)
-            nc.vector.tensor_copy(hid[:, :, t], ha[:].indirect(lists[2][:]))
+            if t == 1:
+                nc.vector.tensor_scalar_max(ha[t][:], acc[t][:], 0.0)
+            else:
+                nc.scalar.activation(ha[t][:], acc[t][:], RELU)
+        for t in range(PACK):
+            if t == PACK - 1:
+                nc.scalar.activation(picked[:, t, :], ha[t][:].indirect(lists[2][:]), COPY)
+            else:
+                nc.vector.tensor_copy(picked[:, t, :], ha[t][:].indirect(lists[2][:]))
         h_codes = tile("h_codes", [P, O], U32)
         h_scales = tile("h_scales", [P, O], U8)
-        nc.vector.quantize_mx(h_codes[:].bitcast(E5M2), h_scales[:], hid[:].rearrange("p c t -> p (c t)"))
+        hid = [tile("hid%d" % h, [P, O // 2, PACK], BF16) for h in range(2)]
+        for h, cols in enumerate(o_halves):
+            nc.vector.tensor_copy(
+                hid[h][:].rearrange("p (c i) t -> p c t i", i=4),
+                picked[:, :, cols].rearrange("p t (c i) -> p c t i", i=4),
+            )
+        for h, cols in enumerate(o_halves):
+            nc.vector.quantize_mx(
+                h_codes[:, cols].bitcast(E5M2), h_scales[:, cols], hid[h][:].rearrange("p c t -> p (c t)")
+            )
 
-        tz_picked = tile("tz_picked", [P, PACK, O], F32)
+        tz_picked = [
+            tile("tz_picked0", [P, 2, O], F32),
+            shared.tile([P, 2, O], F32, name="tz_picked1", align_bytes=64, offset=4096),
+        ]
         for t in range(PACK):
-            nc.scalar.activation(tz_picked[:, t, :], tz_sb[t // 2][:, t % 2, :].indirect(lists[3][:]), COPY)
+            nc.scalar.activation(tz_picked[t // 2][:, t % 2, :], tz_sb[t // 2][:, t % 2, :].indirect(lists[3][:]), COPY)
 
         y = [tile("y%d" % h, [P, 2, O], F32) for h in range(2)]
         y_rows = out_0.rearrange("(p t) o -> p t o", t=PACK)
-        o_halves = [slice(0, O // 2), slice(O // 2, O)]
         y_bf = [tile("y_bf%d" % h, [P, O // 2, PACK], BF16) for h in range(2)]
         for t in range(PACK):
             prod = ps.tile([P, O], F32, name="prod%d" % t)
@@ -186,7 +199,7 @@ def tile_list_pickgaps_relooked_timeslook_pl_kernel(
                 stop=True,
             )
             for cols in o_halves if t == PACK - 1 else [slice(0, O)]:
-                nc.vector.tensor_tensor(y[t // 2][:, t % 2, cols], prod[:, cols], tz_picked[:, t, cols], MULT)
+                nc.vector.tensor_tensor(y[t // 2][:, t % 2, cols], prod[:, cols], tz_picked[t // 2][:, t % 2, cols], MULT)
             if t % 2 == 1:
                 nc.sync.dma_start(y_rows[:, t - 1 : t + 1, :], y[t // 2][:])
                 copy = nc.scalar.copy if t == 1 else nc.vector.tensor_copy

from contextlib import ExitStack

import concourse.mybir as mybir

K, T, J, R, O, N, Z = 1024, 1024, 256, 512, 128, 512, 512
FLOPS = 2 * K * R * J + 2 * R * N * O

F32 = mybir.dt.float32
BF16 = mybir.dt.bfloat16
I32 = mybir.dt.int32
U32 = mybir.dt.uint32
U16 = mybir.dt.uint16
U8 = mybir.dt.uint8
E4M3 = mybir.dt.float8_e4m3fn_x4
E5M2 = mybir.dt.float8_e5m2_x4
E2M1 = mybir.dt.float4_e2m1fn_x4
COPY = mybir.ActivationFunctionType.Copy
RELU = mybir.ActivationFunctionType.Relu
MULT = mybir.AluOpType.mult
SUBTRACT = mybir.AluOpType.subtract

P = 128
PACK = 4
PASSES = K // (P * PACK)


def tile_list_pickgaps_relooked_timeslook_pl_kernel(
    tc, xf, fk, w_words, w_scales, wb_words, wb_scales, tz, offs, offs2, offs3, offs4, out_0, out_1, out_2
):
    nc = tc.nc
    with ExitStack() as ctx:
        sb = ctx.enter_context(tc.tile_pool(name="sb", bufs=1))
        shared = ctx.enter_context(tc.tile_pool(name="shared", bufs=1))
        ps = ctx.enter_context(tc.psum_pool(name="ps", bufs=1))

        def tile(name, shape, dtype):
            return sb.tile(shape, dtype, name=name, align_bytes=64)

        lists = [tile("list%d" % i, list(src.shape), U16) for i, src in enumerate((offs, offs2, offs3, offs4))]
        x_rows = xf.rearrange("(a p t) c -> a t p c", a=PASSES, t=PACK)
        x = [[tile("x%d%d" % (a, t), [P, T], F32) for t in range(PACK)] for a in range(PASSES)]
        fk_sb = tile("fk", [P, PASSES, 2 * PACK], F32)
        w_raw = tile("w_raw", [P, PASSES, 2 * R], U8)
        wb_raw = tile("wb_raw", [P, N], I32)
        ws_raw = tile("ws_raw", [P, PASSES, R], U8)
        wbs_raw = tile("wbs_raw", [P, N], U8)
        tz_rows = tz.rearrange("(p t) z -> p t z", t=PACK)
        tz_sb = [tile("tz%d" % h, [P, 2, Z], F32) for h in range(2)]

        nc.gpsimd.memset(ws_raw[:].bitcast(I32), 0)
        nc.gpsimd.memset(wbs_raw[:].bitcast(I32), 0)

        warm = tile("warm", [P, 1], F32)
        nc.scalar.activation(warm[:], wbs_raw[:, 0:4].bitcast(F32), COPY)
        nc.sync.dma_start(lists[1][:], offs2)
        nc.sync.dma_start(w_raw[:].bitcast(I32), w_words.rearrange("a p b -> p a b").bitcast(I32))
        nc.sync.dma_start(ws_raw[0 : 4].bitcast(I32), w_scales[:, 0 : 4, :].rearrange("a r c -> r a c").bitcast(I32))
        nc.sync.dma_start(ws_raw[32 : 36].bitcast(I32), w_scales[:, 4 : 8, :].rearrange("a r c -> r a c").bitcast(I32))
        nc.sync.dma_start(ws_raw[64 : 68].bitcast(I32), w_scales[:, 8 : 12, :].rearrange("a r c -> r a c").bitcast(I32))
        nc.sync.dma_start(ws_raw[96 : 100].bitcast(I32), w_scales[:, 12 : 16, :].rearrange("a r c -> r a c").bitcast(I32))
        nc.sync.dma_start(x[0][0][:], x_rows[0, 0])
        nc.sync.dma_start(lists[0][:], offs)
        nc.sync.dma_start(x[0][1][:], x_rows[0, 1])
        nc.sync.dma_start(fk_sb[:, :, 0:PACK], fk.rearrange("(a p t) o -> p a (t o)", a=PASSES, t=PACK))
        nc.sync.dma_start(x[0][2][:], x_rows[0, 2])
        nc.sync.dma_start(x[0][3][:], x_rows[0, 3])
        nc.sync.dma_start(x[1][0][:], x_rows[1, 0])
        nc.sync.dma_start(x[1][1][:], x_rows[1, 1])
        nc.sync.dma_start(wbs_raw[0 : 4].bitcast(I32), wb_scales[0, 0 : 4, :].bitcast(I32))
        nc.sync.dma_start(wbs_raw[32 : 36].bitcast(I32), wb_scales[0, 4 : 8, :].bitcast(I32))
        nc.sync.dma_start(wbs_raw[64 : 68].bitcast(I32), wb_scales[0, 8 : 12, :].bitcast(I32))
        nc.sync.dma_start(wbs_raw[96 : 100].bitcast(I32), wb_scales[0, 12 : 16, :].bitcast(I32))
        nc.sync.dma_start(lists[3][:], offs4)
        nc.sync.dma_start(x[1][2][:], x_rows[1, 2])
        nc.sync.dma_start(x[1][3][:], x_rows[1, 3])
        nc.sync.dma_start(wb_raw[:], wb_words[0].rearrange("p c r -> p (c r)").bitcast(I32))
        nc.sync.dma_start(tz_sb[0][:], tz_rows[:, 0 : 2, :])
        nc.sync.dma_start(lists[2][:], offs3)
        nc.sync.dma_start(tz_sb[1][:], tz_rows[:, 2 : 4, :])

        w_dealt = tile("w_dealt", [P, PASSES, PACK, 2 * P], U8)
        ws_dealt = tile("ws_dealt", [P, PASSES, PACK, P], U8)

        acc = [ps.tile([P, J], F32, name="acc%d" % t) for t in range(PACK)]

        halves = [slice(0, J // 2), slice(J // 2, J)]
        list_halves = [slice(0, J // 32), slice(J // 32, J // 16)]

        def first_product(a, u_halves):
            codes = tile("u_codes%d" % a, [P, J], U32)
            scales = tile("u_scales%d" % a, [P, J], U8)
            for cols, u_bf in zip(halves, u_halves):
                nc.vector.quantize_mx(
                    codes[:, cols].bitcast(E4M3), scales[:, cols], u_bf[:].rearrange("p c t -> p (c t)")
                )
            ranges = [slice(0, J)] if a == 0 else halves
            for t in range(PACK):
                for cols in ranges:
                    nc.tensor.matmul_mx(
                        acc[t][:, cols],
                        lhsT=w_dealt[:, a, t, :].bitcast(E2M1),
                        lhsT_scale=ws_dealt[:, a, t, :],
                        rhs=codes[:, cols].bitcast(E4M3),
                        rhs_scale=scales[:, cols],
                        start=(a == 0),
                        stop=(a == PASSES - 1 and cols.stop == J),
                    )

        def gap(a, t):
            second = tile("second%d%d" % (a, t), [P, J], F32)
            d = tile("gap%d%d" % (a, t), [P, J], F32)
            for cols, ent in zip(halves, list_halves):
                nc.scalar.activation(second[:, cols], x[a][t][:].indirect(lists[1][:, ent]), COPY)
            nc.vector.tensor_tensor(d[:, halves[0]], x[a][t][:].indirect(lists[0][:, list_halves[0]]), second[:, halves[0]], SUBTRACT)
            if (a, t) in ((1, 0), (1, 1)):
                first = tile("first%d%d" % (a, t), [P, J // 2], F32)
                nc.scalar.activation(first[:], x[a][t][:].indirect(lists[0][:, list_halves[1]]), COPY)
                nc.vector.tensor_tensor(d[:, halves[1]], first[:], second[:, halves[1]], SUBTRACT)
            else:
                nc.vector.tensor_tensor(d[:, halves[1]], x[a][t][:].indirect(lists[0][:, list_halves[1]]), second[:, halves[1]], SUBTRACT)
            return d

        def factor(a, t):
            return fk_sb[:, a, t : t + 1]

        nc.vector.tensor_copy(
            w_dealt[:].bitcast(U16), w_raw[:].bitcast(U16).rearrange("p a (m t) -> p a t m", t=PACK)
        )
        nc.vector.tensor_copy(ws_dealt[:], ws_raw[:].rearrange("p a (m t) -> p a t m", t=PACK))
        for a in range(PASSES):
            pairs = [tile("pairs%d%d" % (a, h), [P, 2, J // 2, 2], BF16) for h in range(2)]
            for t in range(PACK):
                d = gap(a, t)
                for h, cols in enumerate(halves):
                    nc.vector.tensor_scalar_mul(pairs[h][:, t // 2, :, t % 2], d[:, cols], factor(a, t))
            u = []
            for h in range(2):
                if a == 0:
                    u.append(tile("u0%d" % h, [P, J // 2, PACK], BF16))
                else:
                    u.append(shared.tile([P, J // 2, PACK], BF16, name="u1%d" % h, align_bytes=64, offset=512 + 1024 * h))
                nc.vector.tensor_copy(
                    u[h][:].bitcast(I32), pairs[h][:].bitcast(I32).rearrange("p s c o -> p c (s o)")
                )
            first_product(a, u)
        wb_dealt = shared.tile([P, PACK, P], I32, name="wb_dealt", align_bytes=64, offset=0)
        wbs_dealt = shared.tile([P, PACK, P], U8, name="wbs_dealt", align_bytes=64, offset=2048)
        nc.vector.tensor_copy(wbs_dealt[:], wbs_raw[:].rearrange("p (m t) -> p t m", t=PACK))
        nc.vector.tensor_copy(
            wb_dealt[:].rearrange("p t (c i) -> p c t i", i=4), wb_raw[:].rearrange("p (c i t) -> p c t i", i=4, t=PACK)
        )

        o_halves = [slice(0, O // 2), slice(O // 2, O)]
        picked = tile("picked", [P, PACK, O], F32)
        ha = [tile("ha%d" % t, [P, J], F32) for t in range(PACK - 1)]
        ha.append(shared.tile([P, J], F32, name="ha3", align_bytes=64, offset=4096))
        for t in range(PACK):
            if t == 1:
                nc.vector.tensor_scalar_max(ha[t][:], acc[t][:], 0.0)
            else:
                nc.scalar.activation(ha[t][:], acc[t][:], RELU)
        for t in range(PACK):
            if t == PACK - 1:
                nc.scalar.activation(picked[:, t, :], ha[t][:].indirect(lists[2][:]), COPY)
            else:
                nc.vector.tensor_copy(picked[:, t, :], ha[t][:].indirect(lists[2][:]))
        h_codes = tile("h_codes", [P, O], U32)
        h_scales = tile("h_scales", [P, O], U8)
        hid = [tile("hid%d" % h, [P, O // 2, PACK], BF16) for h in range(2)]
        for h, cols in enumerate(o_halves):
            nc.vector.tensor_copy(
                hid[h][:].rearrange("p (c i) t -> p c t i", i=4),
                picked[:, :, cols].rearrange("p t (c i) -> p c t i", i=4),
            )
        for h, cols in enumerate(o_halves):
            nc.vector.quantize_mx(
                h_codes[:, cols].bitcast(E5M2), h_scales[:, cols], hid[h][:].rearrange("p c t -> p (c t)")
            )

        tz_picked = [
            tile("tz_picked0", [P, 2, O], F32),
            shared.tile([P, 2, O], F32, name="tz_picked1", align_bytes=64, offset=4096),
        ]
        for t in range(PACK):
            nc.scalar.activation(tz_picked[t // 2][:, t % 2, :], tz_sb[t // 2][:, t % 2, :].indirect(lists[3][:]), COPY)

        y = [tile("y%d" % h, [P, 2, O], F32) for h in range(2)]
        y_rows = out_0.rearrange("(p t) o -> p t o", t=PACK)
        y_bf = [tile("y_bf%d" % h, [P, O // 2, PACK], BF16) for h in range(2)]
        for t in range(PACK):
            prod = ps.tile([P, O], F32, name="prod%d" % t)
            nc.tensor.matmul_mx(
                prod[:],
                lhsT=wb_dealt[:, t, :].bitcast(E5M2),
                lhsT_scale=wbs_dealt[:, t, :],
                rhs=h_codes[:].bitcast(E5M2),
                rhs_scale=h_scales[:],
                start=True,
                stop=True,
            )
            for cols in o_halves if t == PACK - 1 else [slice(0, O)]:
                nc.vector.tensor_tensor(y[t // 2][:, t % 2, cols], prod[:, cols], tz_picked[t // 2][:, t % 2, cols], MULT)
            if t % 2 == 1:
                nc.sync.dma_start(y_rows[:, t - 1 : t + 1, :], y[t // 2][:])
                copy = nc.scalar.copy if t == 1 else nc.vector.tensor_copy
                for h, cols in enumerate(o_halves):
                    copy(y_bf[h][:, :, t - 1 : t + 1], y[t // 2][:, :, cols].rearrange("p s c -> p c s"))
        y_codes = tile("y_codes", [P, O], U32)
        y_scales = tile("y_scales", [P, O], U8)
        for h, cols in enumerate(o_halves):
            nc.vector.quantize_mx(
                y_codes[:, cols].bitcast(E4M3), y_scales[:, cols], y_bf[h][:].rearrange("p c t -> p (c t)")
            )
        nc.sync.dma_start(out_1[0].rearrange("p c r -> p (c r)").bitcast(I32), y_codes[:].bitcast(I32))
        for q in range(4):
            queue = nc.scalar if q % 2 == 0 else nc.sync
            queue.dma_start(out_2[0, 4 * q : 4 * q + 4, :].bitcast(I32), y_scales[32 * q : 32 * q + 4, :].bitcast(I32))
